import numpy as np
import ml_dtypes


def mxq(x, axis, fmt="e4m3"):
    dtype, down = {"e4m3": (ml_dtypes.float8_e4m3fn, 7), "e5m2": (ml_dtypes.float8_e5m2, 14)}[fmt]
    v = np.moveaxis(np.asarray(x, np.float32).astype(ml_dtypes.bfloat16).astype(np.float64), axis, -1)
    blocks = v.reshape(v.shape[:-1] + (-1, 32))
    amax = np.abs(blocks).max(-1, keepdims=True)
    byte = np.maximum(np.where(amax > 0, np.frexp(amax)[1] - 1 + 127, 0) - down, 1)
    scale = np.exp2(byte - 127.0)
    codes = (blocks / scale).astype(np.float32).astype(dtype).astype(np.float64)
    return np.moveaxis((codes * scale).reshape(v.shape), -1, axis)


WIDE = False


def mx_kscale(k):
    if not WIDE:
        return np.ones(k)
    levels = np.array([10, -10, 5, -5, 0])
    if k % 512:
        return np.exp2(np.random.permutation(np.resize(levels, k // 32))).repeat(32)
    a = np.empty((k // 512, 16))
    for p in range(k // 512):
        a[p, :8] = np.random.permutation(np.resize(levels, 8))
        for g in range(8):
            far = levels[np.abs(levels - a[p, g]) >= 10]
            a[p, g + 8] = far[np.random.randint(len(far))]
    return np.exp2(a.ravel()).repeat(32)


def f64(x):
    return np.asarray(x).astype(np.float64)


def striped(idx):
    return np.tile(np.asarray(idx).reshape(-1, 16).T, (8, 1)).astype(np.uint16)


def unstriped(offs):
    return offs[:16].T.reshape(-1).astype(np.int64)


E2M1 = np.array([0.0, 0.5, 1.0, 1.5, 2.0, 3.0, 4.0, 6.0, -0.0, -0.5, -1.0, -1.5, -2.0, -3.0, -4.0, -6.0])


def pack_weight(w, fmt):
    k, n = w.shape
    w = f64(np.asarray(w, np.float32).astype(ml_dtypes.bfloat16)).reshape(k // 32, 32, n)
    amax = np.abs(w).max(1)
    if fmt == "e4m3":
        byte = np.frexp(amax)[1] - 1 + 127 - 7
    else:
        mant, ex = np.frexp(amax / 6.0)
        byte = np.where(mant > 0.5, ex, ex - 1) + 127
    byte = np.clip(np.where(amax > 0, byte, 1), 1, 254)
    scaled = (w * np.exp2(127.0 - byte)[:, None, :]).reshape(k, n).astype(np.float32)
    by_word = np.ascontiguousarray(scaled.reshape(k // 512, 128, 4, n).transpose(0, 1, 3, 2))
    if fmt == "e4m3":
        words = by_word.astype(ml_dtypes.float8_e4m3fn).view(np.uint8)
    else:
        c = by_word.astype(ml_dtypes.float4_e2m1fn).view(np.uint8) & 0xF
        words = (c[..., 0::2] | (c[..., 1::2] << 4)).reshape(k // 512, 128, 2 * n)
    return np.ascontiguousarray(words), np.ascontiguousarray(byte.astype(np.uint8).reshape(k // 512, 16, n))


def unpack_weight(words, scales, fmt):
    g, _, n = scales.shape
    words = np.ascontiguousarray(words).reshape(g, 128, n, -1)
    if fmt == "e4m3":
        vals = words.view(ml_dtypes.float8_e4m3fn).astype(np.float64)
    else:
        nib = np.empty((g, 128, n, 4), np.uint8)
        nib[..., 0::2] = words & 0xF
        nib[..., 1::2] = words >> 4
        vals = E2M1[nib]
    vals = vals * np.repeat(np.exp2(scales.astype(np.float64) - 127.0), 8, axis=1)[..., None]
    return vals.transpose(0, 1, 3, 2).reshape(g * 512, n)


D, K, R, T, I, Q, G = 512, 512, 512, 1024, 256, 512, 16


def setup_inputs():
    n = np.random.standard_normal
    idx = np.random.permutation(T)[:I]
    fd = mx_kscale(D)
    fk = mx_kscale(K)
    fq = mx_kscale(Q)
    keysp = pack_weight(n((D, T)) / fd[:, None], "e4m3")
    tabp = pack_weight(n((K, T)) / fk[:, None], "e4m3")
    return {
        "query": (n((D, Q)) * 0.7 / np.sqrt(D) * fd[:, None]).astype(np.float32),
        "keys_words": keysp[0],
        "keys_scales": keysp[1],
        "tab_words": tabp[0],
        "tab_scales": tabp[1],
        "w1": (n((K, R)) * 1 / np.sqrt(K) * fk[:, None]).astype(np.float32),
        "share": (np.random.uniform(0.4, 1.0, (R, 1))).astype(np.float32),
        "qs": (np.random.uniform(4.0, 16.0, (Q, 1)) * fq[:, None]).astype(np.float32),
        "grows": (n((Q, R)) / fq[:, None]).astype(np.float32),
        "sg": (np.random.uniform(0.5, 2.0, (1, I))).astype(np.float32),
        "old": (0.4 * n((R, I))).astype(np.float32),
        "offs": striped(idx),
    }


def reference(query, keys_words, keys_scales, tab_words, tab_scales, w1, share, qs, grows, sg, old, offs):
    idx = unstriped(offs)
    keysu = unpack_weight(keys_words, keys_scales, "e4m3")
    tabu = unpack_weight(tab_words, tab_scales, "e4m3")
    queryq = mxq(f64(query), 0, "e4m3")
    keysidxg = keysu[:, idx]
    a = queryq.T @ keysidxg
    p = np.exp(a - np.max(a, axis=1, keepdims=True))
    z = np.sum(p, axis=1, keepdims=True)
    w = p / z
    wq = w * f64(qs)
    w1q = mxq(f64(w1), 0, "e4m3")
    tabidxg = tabu[:, idx]
    zh = w1q.T @ tabidxg
    mz = zh.reshape(R, G, I // G).mean(axis=2)
    mzr = np.repeat(mz, I // G, axis=1)
    hv = np.tanh(zh - mzr * f64(share))
    growsq = mxq(f64(grows), 0, "e4m3")
    wqq = mxq(wq, 0, "e4m3")
    c0 = growsq.T @ wqq
    dmzr = c0 * (1.0 - np.square(hv)) * (-1.0) * f64(share)
    dmz = dmzr.reshape(R, G, I // G).sum(axis=2)
    e1 = dmz / 16.0
    r1 = np.repeat(e1, I // G, axis=1)
    dzh = c0 * (1.0 - np.square(hv)) + r1
    y = dzh * f64(sg) + f64(old)
    return y

@@ -1,0 +1,211 @@
+from contextlib import ExitStack
+
+import concourse.mybir as mybir
+from concourse.masks import make_identity
+
+F32 = mybir.dt.float32
+BF16 = mybir.dt.bfloat16
+I32 = mybir.dt.int32
+U32 = mybir.dt.uint32
+U16 = mybir.dt.uint16
+U8 = mybir.dt.uint8
+FP8X4 = mybir.dt.float8_e4m3fn_x4
+ALU = mybir.AluOpType
+ACT = mybir.ActivationFunctionType
+AXIS_X = mybir.AxisListType.X
+
+P = 128
+T = 1024
+SLOTS = 256
+PAGE = 16
+PAGES = SLOTS // PAGE
+FLOPS = 3 * 2 * 512 * 512 * 256
+
+
+def tile_attend_bzcentred_soft_kernel(tc, query, keys_words, keys_scales, tab_words, tab_scales, w1, share, qs, grows, sg, old, offs, out):
+    nc = tc.nc
+    with ExitStack() as ctx:
+        sb = ctx.enter_context(tc.tile_pool(name="sb", bufs=1))
+        ps = ctx.enter_context(tc.psum_pool(name="ps", bufs=1))
+
+        def load_scales(name, scales):
+            plane = sb.tile([P, T], U8, name=name, align_bytes=64)
+            rows = scales[0].bitcast(I32)
+            for quad in range(4):
+                nc.sync.dma_start(
+                    out=plane[32 * quad : 32 * quad + 32, :].bitcast(I32),
+                    in_=rows[4 * quad : 4 * quad + 4, :].unsqueeze(0).broadcast_to([8, 4, T // 4]),
+                )
+            return plane
+
+        def load_words(name, words):
+            pool_words = sb.tile([P, T], U32, name=name, align_bytes=64)
+            nc.sync.dma_start(out=pool_words[:].bitcast(I32), in_=words[0].rearrange("p n t -> p (n t)").bitcast(I32))
+            return pool_words
+
+        def gather(name, window, dtype):
+            picked = sb.tile([P, SLOTS], dtype, name=name, align_bytes=64)
+            nc.vector.tensor_copy(out=picked[:], in_=window[:].indirect(offsets[:]))
+            return picked
+
+        def quantize(name, values, width):
+            codes = sb.tile([P, width], U32, name=name + "_codes", align_bytes=64)
+            scales = sb.tile([P, width], U8, name=name + "_scales", align_bytes=64)
+            nc.vector.quantize_mx(out=codes[:].bitcast(FP8X4), scales=scales[:], in_=values)
+            return codes, scales
+
+        def product(dst, stationary, col, moving):
+            nc.tensor.matmul_mx(
+                out=dst,
+                lhsT=stationary[0][:, col * P : (col + 1) * P].bitcast(FP8X4),
+                lhsT_scale=stationary[1][:, col * P : (col + 1) * P],
+                rhs=moving[0][:].bitcast(FP8X4),
+                rhs_scale=moving[1][:],
+                start=True,
+                stop=True,
+            )
+
+        def interleave_half(name, raw_half):
+            packed = sb.tile([P, 2, P, 4], BF16, name=name, align_bytes=64)
+            dst = packed[:].rearrange("p e (m n) j -> p m j n e", n=2)
+            src = raw_half.rearrange("p j (m n e) -> p m j n e", n=2, e=2)
+            for m0 in (0, 32):
+                nc.scalar.copy(out=dst[:, m0 : m0 + 32], in_=src[:, m0 : m0 + 32])
+            return packed
+
+        offsets = sb.tile([P, SLOTS // 16], U16, name="offsets")
+        nc.sync.dma_start(offsets[:], offs)
+        key_plane = load_scales("key_plane", keys_scales)
+        q_raw = sb.tile([P, 4, 512], F32, name="q_raw")
+        nc.sync.dma_start(out=q_raw[:], in_=query.rearrange("(p j) q -> p j q", j=4))
+        key_pool = load_words("key_pool", keys_words)
+        tab_pool = load_words("tab_pool", tab_words)
+        tab_plane = load_scales("tab_plane", tab_scales)
+        w_raw = sb.tile([P, 4, 512], F32, name="w_raw")
+        nc.sync.dma_start(out=w_raw[:], in_=w1.rearrange("(p j) r -> p j r", j=4))
+        qs_sb = sb.tile([P, 4], F32, name="qs_sb")
+        nc.sync.dma_start(out=qs_sb[:], in_=qs.rearrange("(p t) o -> p (t o)", t=4))
+        sg_col = sb.tile([P, 2], F32, name="sg_col")
+        nc.sync.dma_start(out=sg_col[:], in_=sg.rearrange("o (p e) -> p (o e)", e=2))
+        share_sb = sb.tile([P, 2, 2], F32, name="share_sb")
+        nc.sync.dma_start(out=share_sb[:], in_=share.rearrange("(h p e) o -> p h (e o)", h=2, e=2))
+        g_raw = []
+        for h in range(2):
+            half = sb.tile([P, 4, 256], F32, name="g_raw%d" % h)
+            nc.sync.dma_start(out=half[:], in_=grows[:, 256 * h : 256 * (h + 1)].rearrange("(p j) r -> p j r", j=4))
+            g_raw.append(half)
+        old_sb = sb.tile([P, 2, 2 * SLOTS], F32, name="old_sb")
+        nc.sync.dma_start(out=old_sb[:], in_=old.rearrange("(h p e) i -> p h (e i)", h=2, e=2))
+
+        warm = sb.tile([P, 1], F32, name="warm")
+        warm_out = sb.tile([P, 1], F32, name="warm_out")
+        nc.vector.memset(warm[:], 0.0)
+        nc.scalar.activation(out=warm_out[:], in_=warm[:], func=ACT.Exp)
+        ident = sb.tile([P, P], F32, name="ident")
+        make_identity(nc, ident[:])
+
+        key_scale = gather("key_scale", key_plane, U8)
+        q_packed = sb.tile([P, 4, P, 4], BF16, name="q_packed", align_bytes=64)
+        q_dst = q_packed[:].rearrange("p t m j -> p m j t")
+        q_src = q_raw[:].rearrange("p j (m t) -> p m j t", t=4)
+        split = 48
+        nc.scalar.copy(out=q_dst[:, :split], in_=q_src[:, :split])
+        nc.vector.tensor_copy(out=q_dst[:, split:], in_=q_src[:, split:])
+        q_mx = quantize("q", q_packed[:].rearrange("p t m j -> p (t m j)"), 512)
+        key_mx = (gather("key_words", key_pool, U32), key_scale)
+        scores = [ps.tile([P, 2, SLOTS], F32, name="scores%d" % b) for b in range(2)]
+        for t in range(4):
+            product(scores[t // 2][:, t % 2, :], q_mx, t, key_mx)
+        tab_mx = (gather("tab_words", tab_pool, U32), gather("tab_scale", tab_plane, U8))
+
+        expd = sb.tile([P, 4, SLOTS], F32, name="expd")
+        weights = sb.tile([P, 4, SLOTS], BF16, name="weights")
+        for b in range(2):
+            neg_max = sb.tile([P, 2], F32, name="neg_max%d" % b)
+            nc.vector.tensor_reduce(out=neg_max[:], in_=scores[b][:], axis=AXIS_X, op=ALU.max, negate=True)
+            row_sum = sb.tile([P, 2], F32, name="row_sum%d" % b)
+            for e in range(2):
+                nc.scalar.activation(
+                    out=expd[:, 2 * b + e, :], in_=scores[b][:, e, :], func=ACT.Exp,
+                    bias=neg_max[:, e : e + 1], accum_out=row_sum[:, e : e + 1],
+                )
+            inv_sum = sb.tile([P, 2], F32, name="inv_sum%d" % b)
+            nc.vector.reciprocal(out=inv_sum[:], in_=row_sum[:])
+            for e in range(2):
+                t = 2 * b + e
+                nc.vector.tensor_scalar(
+                    out=weights[:, t, :], in0=expd[:, t, :], scalar1=inv_sum[:, e : e + 1], scalar2=qs_sb[:, t : t + 1],
+                    op0=ALU.mult, op1=ALU.mult,
+                )
+        wq_packed = sb.tile([P, SLOTS, 4], BF16, name="wq_packed", align_bytes=64)
+        nc.vector.tensor_copy(
+            out=wq_packed[:].rearrange("p (c i) t -> p c t i", i=4),
+            in_=weights[:].rearrange("p t (c i) -> p c t i", i=4),
+        )
+        wq_mx = quantize("wq", wq_packed[:].rearrange("p i t -> p (i t)"), SLOTS)
+
+        neg_share = sb.tile([P, 2, 2], F32, name="neg_share")
+        nc.vector.tensor_scalar(out=neg_share[:], in0=share_sb[:], scalar1=-1.0 / PAGE, scalar2=None, op0=ALU.mult)
+
+        def centre(name, h, values):
+            sums = sb.tile([P, 2, PAGES], F32, name=name + "_sums")
+            nc.vector.tensor_reduce(
+                out=sums[:].rearrange("p e g -> p (e g)"), in_=values.rearrange("p e (g j) -> p (e g) j", j=PAGE),
+                axis=AXIS_X, op=ALU.add,
+            )
+            centred = sb.tile([P, 2, SLOTS], F32, name=name)
+            for e in range(2):
+                nc.vector.scalar_tensor_tensor(
+                    out=centred[:, e, :].rearrange("p (g j) -> p g j", j=PAGE),
+                    in0=sums[:, e, :].unsqueeze(2).broadcast_to([P, PAGES, PAGE]),
+                    scalar=neg_share[:, h, e : e + 1],
+                    in1=values[:, e, :].rearrange("p (g j) -> p g j", j=PAGE),
+                    op0=ALU.mult, op1=ALU.add,
+                )
+            return centred
+
+        squares = []
+        for h in range(2):
+            w_packed = interleave_half("w_packed%d" % h, w_raw[:, :, 256 * h : 256 * (h + 1)])
+            w_mx = quantize("w%d" % h, w_packed[:].rearrange("p e m j -> p (e m j)"), 256)
+            sums_zh = ps.tile([P, 2, SLOTS], F32, name="zh%d" % h)
+            for e in range(2):
+                product(sums_zh[:, e, :], w_mx, e, tab_mx)
+            pre = centre("pre%d" % h, h, sums_zh[:])
+            hv = sb.tile([P, 2, SLOTS], F32, name="hv%d" % h)
+            nc.scalar.activation(out=hv[:], in_=pre[:], func=ACT.Tanh)
+            sq = sb.tile([P, 2, SLOTS], F32, name="sq%d" % h)
+            nc.scalar.activation(out=sq[:], in_=hv[:], func=ACT.Square)
+            squares.append(sq)
+
+        gain = ps.tile([P, 2, P], F32, name="gain")
+        for e in range(2):
+            nc.tensor.transpose(gain[:, e, :], sg_col[:, e : e + 1].to_broadcast([P, P]), ident[:])
+
+        grads = []
+        for h in range(2):
+            g_packed = interleave_half("g_packed%d" % h, g_raw[h][:])
+            g_mx = quantize("g%d" % h, g_packed[:].rearrange("p e m j -> p (e m j)"), 256)
+            c0 = ps.tile([P, 2, SLOTS], F32, name="c0_%d" % h)
+            for e in range(2):
+                product(c0[:, e, :], g_mx, e, wq_mx)
+            grads.append(c0)
+
+        for h in range(2):
+            c0 = grads[h]
+            neg_u = sb.tile([P, 2, SLOTS], F32, name="neg_u%d" % h)
+            nc.vector.scalar_tensor_tensor(
+                out=neg_u[:].rearrange("p e i -> p (e i)"), in0=squares[h][:].rearrange("p e i -> p (e i)"), scalar=1.0,
+                in1=c0[:].rearrange("p e i -> p (e i)"), op0=ALU.subtract, op1=ALU.mult,
+            )
+            neg_dzh = centre("neg_dzh%d" % h, h, neg_u[:])
+            gained = sb.tile([P, 2, SLOTS], F32, name="gained%d" % h)
+            nc.vector.tensor_tensor(
+                out=gained[:].rearrange("p e (n f) -> p e n f", f=2),
+                in0=neg_dzh[:].rearrange("p e (n f) -> p e n f", f=2),
+                in1=gain[:].rearrange("p f n -> p n f").unsqueeze(1).broadcast_to([P, 2, P, 2]),
+                op=ALU.mult,
+            )
+            result = sb.tile([P, 2 * SLOTS], F32, name="result%d" % h)
+            nc.vector.tensor_tensor(out=result[:], in0=old_sb[:, h, :], in1=gained[:].rearrange("p e i -> p (e i)"), op=ALU.subtract)
+            nc.sync.dma_start(out=out[256 * h : 256 * (h + 1), :].rearrange("(p e) i -> p (e i)", e=2), in_=result[:])

@@ -28,11 +28,11 @@ def tile_attend_bzcentred_soft_kernel(tc, query, keys_words, keys_scales, tab_wo
         sb = ctx.enter_context(tc.tile_pool(name="sb", bufs=1))
         ps = ctx.enter_context(tc.psum_pool(name="ps", bufs=1))
 
-        def load_scales(name, scales):
+        def load_scales(name, scales, queue):
             plane = sb.tile([P, T], U8, name=name, align_bytes=64)
             rows = scales[0].bitcast(I32)
             for quad in range(4):
-                nc.sync.dma_start(
+                queue.dma_start(
                     out=plane[32 * quad : 32 * quad + 32, :].bitcast(I32),
                     in_=rows[4 * quad : 4 * quad + 4, :].unsqueeze(0).broadcast_to([8, 4, T // 4]),
                 )
@@ -43,13 +43,18 @@ def tile_attend_bzcentred_soft_kernel(tc, query, keys_words, keys_scales, tab_wo
             nc.sync.dma_start(out=pool_words[:].bitcast(I32), in_=words[0].rearrange("p n t -> p (n t)").bitcast(I32))
             return pool_words
 
-        def gather(name, window, dtype):
-            picked = sb.tile([P, SLOTS], dtype, name=name, align_bytes=64)
+        def load_half(name, matrix, h):
+            half = sb.tile([P, 4, 256], F32, name=name, align_bytes=64)
+            nc.sync.dma_start(out=half[:], in_=matrix[:, 256 * h : 256 * (h + 1)].rearrange("(p j) r -> p j r", j=4))
+            return half
+
+        def gather(name, window, dtype, tag=None):
+            picked = sb.tile([P, SLOTS], dtype, name=name, tag=tag or name, align_bytes=64)
             nc.vector.tensor_copy(out=picked[:], in_=window[:].indirect(offsets[:]))
             return picked
 
-        def quantize(name, values, width):
-            codes = sb.tile([P, width], U32, name=name + "_codes", align_bytes=64)
+        def quantize(name, values, width, tag=None):
+            codes = sb.tile([P, width], U32, name=name + "_codes", tag=tag or name + "_codes", align_bytes=64)
             scales = sb.tile([P, width], U8, name=name + "_scales", align_bytes=64)
             nc.vector.quantize_mx(out=codes[:].bitcast(FP8X4), scales=scales[:], in_=values)
             return codes, scales
@@ -65,8 +70,8 @@ def tile_attend_bzcentred_soft_kernel(tc, query, keys_words, keys_scales, tab_wo
                 stop=True,
             )
 
-        def interleave_half(name, raw_half):
-            packed = sb.tile([P, 2, P, 4], BF16, name=name, align_bytes=64)
+        def interleave_half(name, raw_half, tag=None):
+            packed = sb.tile([P, 2, P, 4], BF16, name=name, tag=tag or name, align_bytes=64)
             dst = packed[:].rearrange("p e (m n) j -> p m j n e", n=2)
             src = raw_half.rearrange("p j (m n e) -> p m j n e", n=2, e=2)
             for m0 in (0, 32):
@@ -75,25 +80,21 @@ def tile_attend_bzcentred_soft_kernel(tc, query, keys_words, keys_scales, tab_wo
 
         offsets = sb.tile([P, SLOTS // 16], U16, name="offsets")
         nc.sync.dma_start(offsets[:], offs)
-        key_plane = load_scales("key_plane", keys_scales)
-        q_raw = sb.tile([P, 4, 512], F32, name="q_raw")
-        nc.sync.dma_start(out=q_raw[:], in_=query.rearrange("(p j) q -> p j q", j=4))
+        key_plane = load_scales("key_plane", keys_scales, nc.sync)
+        q_raw = [load_half("q_raw%d" % h, query, h) for h in range(2)]
         key_pool = load_words("key_pool", keys_words)
+        w_raw = [load_half("w_raw0", w1, 0)]
+        tab_plane = load_scales("tab_plane", tab_scales, nc.sync)
+        w_raw.append(load_half("w_raw1", w1, 1))
         tab_pool = load_words("tab_pool", tab_words)
-        tab_plane = load_scales("tab_plane", tab_scales)
-        w_raw = sb.tile([P, 4, 512], F32, name="w_raw")
-        nc.sync.dma_start(out=w_raw[:], in_=w1.rearrange("(p j) r -> p j r", j=4))
         qs_sb = sb.tile([P, 4], F32, name="qs_sb")
         nc.sync.dma_start(out=qs_sb[:], in_=qs.rearrange("(p t) o -> p (t o)", t=4))
-        sg_col = sb.tile([P, 2], F32, name="sg_col")
-        nc.sync.dma_start(out=sg_col[:], in_=sg.rearrange("o (p e) -> p (o e)", e=2))
         share_sb = sb.tile([P, 2, 2], F32, name="share_sb")
         nc.sync.dma_start(out=share_sb[:], in_=share.rearrange("(h p e) o -> p h (e o)", h=2, e=2))
-        g_raw = []
-        for h in range(2):
-            half = sb.tile([P, 4, 256], F32, name="g_raw%d" % h)
-            nc.sync.dma_start(out=half[:], in_=grows[:, 256 * h : 256 * (h + 1)].rearrange("(p j) r -> p j r", j=4))
-            g_raw.append(half)
+        g_raw = [load_half("g_raw0", grows, 0)]
+        sg_col = sb.tile([P, 2], F32, name="sg_col")
+        nc.sync.dma_start(out=sg_col[:], in_=sg.rearrange("o (p e) -> p (o e)", e=2))
+        g_raw.append(load_half("g_raw1", grows, 1))
         old_sb = sb.tile([P, 2, 2 * SLOTS], F32, name="old_sb")
         nc.sync.dma_start(out=old_sb[:], in_=old.rearrange("(h p e) i -> p h (e i)", h=2, e=2))
 
@@ -104,55 +105,21 @@ def tile_attend_bzcentred_soft_kernel(tc, query, keys_words, keys_scales, tab_wo
         ident = sb.tile([P, P], F32, name="ident")
         make_identity(nc, ident[:])
 
-        key_scale = gather("key_scale", key_plane, U8)
-        q_packed = sb.tile([P, 4, P, 4], BF16, name="q_packed", align_bytes=64)
-        q_dst = q_packed[:].rearrange("p t m j -> p m j t")
-        q_src = q_raw[:].rearrange("p j (m t) -> p m j t", t=4)
-        split = 48
-        nc.scalar.copy(out=q_dst[:, :split], in_=q_src[:, :split])
-        nc.vector.tensor_copy(out=q_dst[:, split:], in_=q_src[:, split:])
-        q_mx = quantize("q", q_packed[:].rearrange("p t m j -> p (t m j)"), 512)
-        key_mx = (gather("key_words", key_pool, U32), key_scale)
-        scores = [ps.tile([P, 2, SLOTS], F32, name="scores%d" % b) for b in range(2)]
-        for t in range(4):
-            product(scores[t // 2][:, t % 2, :], q_mx, t, key_mx)
-        tab_mx = (gather("tab_words", tab_pool, U32), gather("tab_scale", tab_plane, U8))
-
-        expd = sb.tile([P, 4, SLOTS], F32, name="expd")
-        weights = sb.tile([P, 4, SLOTS], BF16, name="weights")
-        for b in range(2):
-            neg_max = sb.tile([P, 2], F32, name="neg_max%d" % b)
-            nc.vector.tensor_reduce(out=neg_max[:], in_=scores[b][:], axis=AXIS_X, op=ALU.max, negate=True)
-            row_sum = sb.tile([P, 2], F32, name="row_sum%d" % b)
-            for e in range(2):
-                nc.scalar.activation(
-                    out=expd[:, 2 * b + e, :], in_=scores[b][:, e, :], func=ACT.Exp,
-                    bias=neg_max[:, e : e + 1], accum_out=row_sum[:, e : e + 1],
-                )
-            inv_sum = sb.tile([P, 2], F32, name="inv_sum%d" % b)
-            nc.vector.reciprocal(out=inv_sum[:], in_=row_sum[:])
-            for e in range(2):
-                t = 2 * b + e
-                nc.vector.tensor_scalar(
-                    out=weights[:, t, :], in0=expd[:, t, :], scalar1=inv_sum[:, e : e + 1], scalar2=qs_sb[:, t : t + 1],
-                    op0=ALU.mult, op1=ALU.mult,
-                )
-        wq_packed = sb.tile([P, SLOTS, 4], BF16, name="wq_packed", align_bytes=64)
-        nc.vector.tensor_copy(
-            out=wq_packed[:].rearrange("p (c i) t -> p c t i", i=4),
-            in_=weights[:].rearrange("p t (c i) -> p c t i", i=4),
-        )
-        wq_mx = quantize("wq", wq_packed[:].rearrange("p i t -> p (i t)"), SLOTS)
+        def merged(ap):
+            return ap.rearrange("p e m j -> p (e m j)")
 
         neg_share = sb.tile([P, 2, 2], F32, name="neg_share")
-        nc.vector.tensor_scalar(out=neg_share[:], in0=share_sb[:], scalar1=-1.0 / PAGE, scalar2=None, op0=ALU.mult)
+        nc.gpsimd.tensor_scalar(out=neg_share[:], in0=share_sb[:], scalar1=-1.0 / PAGE, scalar2=0.0, op0=ALU.mult, op1=ALU.add)
 
-        def centre(name, h, values):
-            sums = sb.tile([P, 2, PAGES], F32, name=name + "_sums")
+        def page_sums(name, values):
+            sums = sb.tile([P, 2, PAGES], F32, name=name)
             nc.vector.tensor_reduce(
                 out=sums[:].rearrange("p e g -> p (e g)"), in_=values.rearrange("p e (g j) -> p (e g) j", j=PAGE),
                 axis=AXIS_X, op=ALU.add,
             )
+            return sums
+
+        def centre(name, h, values, sums):
             centred = sb.tile([P, 2, SLOTS], F32, name=name)
             for e in range(2):
                 nc.vector.scalar_tensor_tensor(
@@ -164,48 +131,114 @@ def tile_attend_bzcentred_soft_kernel(tc, query, keys_words, keys_scales, tab_wo
                 )
             return centred
 
-        squares = []
-        for h in range(2):
-            w_packed = interleave_half("w_packed%d" % h, w_raw[:, :, 256 * h : 256 * (h + 1)])
-            w_mx = quantize("w%d" % h, w_packed[:].rearrange("p e m j -> p (e m j)"), 256)
+
+        def layer_sums(h, w_mx):
             sums_zh = ps.tile([P, 2, SLOTS], F32, name="zh%d" % h)
             for e in range(2):
                 product(sums_zh[:, e, :], w_mx, e, tab_mx)
-            pre = centre("pre%d" % h, h, sums_zh[:])
-            hv = sb.tile([P, 2, SLOTS], F32, name="hv%d" % h)
-            nc.scalar.activation(out=hv[:], in_=pre[:], func=ACT.Tanh)
-            sq = sb.tile([P, 2, SLOTS], F32, name="sq%d" % h)
-            nc.scalar.activation(out=sq[:], in_=hv[:], func=ACT.Square)
-            squares.append(sq)
+            return sums_zh
 
-        gain = ps.tile([P, 2, P], F32, name="gain")
+        key_scale = gather("key_scale", key_plane, U8)
+        q_packed = sb.tile([P, 4, P, 4], BF16, name="q_packed", align_bytes=64)
+        q_dst = q_packed[:].rearrange("p t m j -> p m j t")
+        q_src = [half[:].rearrange("p j (m t) -> p m j t", t=4) for half in q_raw]
+        nc.scalar.copy(out=q_dst[:, :64], in_=q_src[0])
+        nc.vector.tensor_copy(out=q_dst[:, 64:], in_=q_src[1])
+        q_mx = [quantize("q0", merged(q_packed[:, 0:2]), 256)]
+        key_mx = (gather("key_words", key_pool, U32), key_scale)
+        q_mx.append(quantize("q1", merged(q_packed[:, 2:4]), 256))
+        scores = [ps.tile([P, 2, SLOTS], F32, name="scores%d" % b) for b in range(2)]
+        for t in range(4):
+            product(scores[t // 2][:, t % 2, :], q_mx[t // 2], t % 2, key_mx)
+        tab_scale = gather("tab_scale", tab_plane, U8)
+        w_packed = [interleave_half("w_packed%d" % h, w_raw[h][:]) for h in range(2)]
+
+        expd = sb.tile([P, 4, SLOTS], F32, name="expd", tag="w_raw1", align_bytes=64)
+        row_sums = []
+        for b in range(2):
+            neg_max = sb.tile([P, 2], F32, name="neg_max%d" % b, tag=("tab_plane", "neg_max1")[b], align_bytes=64)
+            nc.vector.tensor_reduce(out=neg_max[:], in_=scores[b][:], axis=AXIS_X, op=ALU.max, negate=True)
+            row_sum = sb.tile([P, 2], F32, name="row_sum%d" % b)
+            for e in range(2):
+                nc.scalar.activation(
+                    out=expd[:, 2 * b + e, :], in_=scores[b][:, e, :], func=ACT.Exp,
+                    bias=neg_max[:, e : e + 1], accum_out=row_sum[:, e : e + 1],
+                )
+            row_sums.append(row_sum)
+
+        weights = sb.tile([P, 4, SLOTS], BF16, name="weights")
+
+        def invert(b, tag):
+            inv_sum = sb.tile([P, 2], F32, name="inv_sum%d" % b, tag=tag, align_bytes=64)
+            nc.vector.reciprocal(out=inv_sum[:], in_=row_sums[b][:])
+            return inv_sum
+
+        def normalise(b, inv_sum):
+            for e in range(2):
+                t = 2 * b + e
+                nc.vector.tensor_scalar(
+                    out=weights[:, t, :], in0=expd[:, t, :], scalar1=inv_sum[:, e : e + 1], scalar2=qs_sb[:, t : t + 1],
+                    op0=ALU.mult, op1=ALU.mult,
+                )
+
+        w_mx0 = quantize("w0", merged(w_packed[0][:]), 256)
+        tab_mx = (gather("tab_words", tab_pool, U32), tab_scale)
+        zh = [layer_sums(0, w_mx0), layer_sums(1, quantize("w1", merged(w_packed[1][:]), 256))]
+        normalise(0, invert(0, "tab_pool"))
+        zh_sums = [page_sums("zh_sums0", zh[0][:])]
+        inv_sum1 = invert(1, "inv_sum1")
+        zh_sums.append(page_sums("zh_sums1", zh[1][:]))
+        normalise(1, inv_sum1)
+        pre = [centre("pre0", 0, zh[0][:], zh_sums[0])]
+        wq_packed = sb.tile([P, SLOTS, 4], BF16, name="wq_packed", align_bytes=64)
+        nc.vector.tensor_copy(
+            out=wq_packed[:].rearrange("p (c i) t -> p c t i", i=4),
+            in_=weights[:].rearrange("p t (c i) -> p c t i", i=4),
+        )
+
+        g_packed = [interleave_half("g_packed%d" % h, g_raw[h][:], ("neg_max1", None)[h]) for h in range(2)]
+        g_mx = [quantize("g0", merged(g_packed[0][:]), 256)]
+        wq_mx = quantize("wq", wq_packed[:].rearrange("p i t -> p (i t)"), SLOTS)
+        pre.append(centre("pre1", 1, zh[1][:], zh_sums[1]))
+        g_mx.append(quantize("g1", merged(g_packed[1][:]), 256))
+
+        gain = ps.tile([P, 2, P], F32, name="gain", tag="scores1")
         for e in range(2):
             nc.tensor.transpose(gain[:, e, :], sg_col[:, e : e + 1].to_broadcast([P, P]), ident[:])
-
         grads = []
         for h in range(2):
-            g_packed = interleave_half("g_packed%d" % h, g_raw[h][:])
-            g_mx = quantize("g%d" % h, g_packed[:].rearrange("p e m j -> p (e m j)"), 256)
             c0 = ps.tile([P, 2, SLOTS], F32, name="c0_%d" % h)
             for e in range(2):
-                product(c0[:, e, :], g_mx, e, wq_mx)
+                product(c0[:, e, :], g_mx[h], e, wq_mx)
             grads.append(c0)
 
+        squares = []
+        hv_all = sb.tile([P, 2, 2, SLOTS], F32, name="hv", tag="g_raw1", align_bytes=64)
         for h in range(2):
-            c0 = grads[h]
-            neg_u = sb.tile([P, 2, SLOTS], F32, name="neg_u%d" % h)
+            hv = hv_all[:, h]
+            nc.scalar.activation(out=hv, in_=pre[h][:], func=ACT.Tanh)
+            squares.append(sb.tile([P, 2, SLOTS], F32, name="sq%d" % h))
+            nc.scalar.activation(out=squares[h][:], in_=hv, func=ACT.Square)
+
+        neg_u = []
+        for h in range(2):
+            neg_u.append(sb.tile([P, 2, SLOTS], F32, name="neg_u%d" % h))
             nc.vector.scalar_tensor_tensor(
-                out=neg_u[:].rearrange("p e i -> p (e i)"), in0=squares[h][:].rearrange("p e i -> p (e i)"), scalar=1.0,
-                in1=c0[:].rearrange("p e i -> p (e i)"), op0=ALU.subtract, op1=ALU.mult,
+                out=neg_u[h][:].rearrange("p e i -> p (e i)"), in0=squares[h][:].rearrange("p e i -> p (e i)"), scalar=1.0,
+                in1=grads[h][:].rearrange("p e i -> p (e i)"), op0=ALU.subtract, op1=ALU.mult,
             )
-            neg_dzh = centre("neg_dzh%d" % h, h, neg_u[:])
-            gained = sb.tile([P, 2, SLOTS], F32, name="gained%d" % h)
+        u_sums = [page_sums("u_sums%d" % h, neg_u[h][:]) for h in range(2)]
+        neg_dzh = [centre("neg_dzh%d" % h, h, neg_u[h][:], u_sums[h]) for h in range(2)]
+        gained = []
+        for h in range(2):
+            gained.append(sb.tile([P, 2, SLOTS], F32, name="gained%d" % h))
             nc.vector.tensor_tensor(
-                out=gained[:].rearrange("p e (n f) -> p e n f", f=2),
-                in0=neg_dzh[:].rearrange("p e (n f) -> p e n f", f=2),
+                out=gained[h][:].rearrange("p e (n f) -> p e n f", f=2),
+                in0=neg_dzh[h][:].rearrange("p e (n f) -> p e n f", f=2),
                 in1=gain[:].rearrange("p f n -> p n f").unsqueeze(1).broadcast_to([P, 2, P, 2]),
                 op=ALU.mult,
             )
+        for h in range(2):
             result = sb.tile([P, 2 * SLOTS], F32, name="result%d" % h)
-            nc.vector.tensor_tensor(out=result[:], in0=old_sb[:, h, :], in1=gained[:].rearrange("p e i -> p (e i)"), op=ALU.subtract)
+            nc.vector.tensor_tensor(out=result[:], in0=old_sb[:, h, :], in1=gained[h][:].rearrange("p e i -> p (e i)"), op=ALU.subtract)
             nc.sync.dma_start(out=out[256 * h : 256 * (h + 1), :].rearrange("(p e) i -> p (e i)", e=2), in_=result[:])

@@ -48,6 +48,11 @@ def tile_attend_bzcentred_soft_kernel(tc, query, keys_words, keys_scales, tab_wo
             nc.sync.dma_start(out=half[:], in_=matrix[:, 256 * h : 256 * (h + 1)].rearrange("(p j) r -> p j r", j=4))
             return half
 
+        def load_whole(name, matrix):
+            whole = sb.tile([P, 4, 512], F32, name=name, align_bytes=64)
+            nc.sync.dma_start(out=whole[:], in_=matrix.rearrange("(p j) r -> p j r", j=4))
+            return whole
+
         def gather(name, window, dtype, tag=None):
             picked = sb.tile([P, SLOTS], dtype, name=name, tag=tag or name, align_bytes=64)
             nc.vector.tensor_copy(out=picked[:], in_=window[:].indirect(offsets[:]))
@@ -74,14 +79,13 @@ def tile_attend_bzcentred_soft_kernel(tc, query, keys_words, keys_scales, tab_wo
             packed = sb.tile([P, 2, P, 4], BF16, name=name, tag=tag or name, align_bytes=64)
             dst = packed[:].rearrange("p e (m n) j -> p m j n e", n=2)
             src = raw_half.rearrange("p j (m n e) -> p m j n e", n=2, e=2)
-            for m0 in (0, 32):
-                nc.scalar.copy(out=dst[:, m0 : m0 + 32], in_=src[:, m0 : m0 + 32])
+            nc.scalar.copy(out=dst, in_=src)
             return packed
 
         offsets = sb.tile([P, SLOTS // 16], U16, name="offsets")
         nc.sync.dma_start(offsets[:], offs)
         key_plane = load_scales("key_plane", keys_scales, nc.sync)
-        q_raw = [load_half("q_raw%d" % h, query, h) for h in range(2)]
+        q_raw = load_whole("q_raw", query)
         key_pool = load_words("key_pool", keys_words)
         w_raw = [load_half("w_raw0", w1, 0)]
         tab_plane = load_scales("tab_plane", tab_scales, nc.sync)
@@ -89,14 +93,13 @@ def tile_attend_bzcentred_soft_kernel(tc, query, keys_words, keys_scales, tab_wo
         tab_pool = load_words("tab_pool", tab_words)
         qs_sb = sb.tile([P, 4], F32, name="qs_sb")
         nc.sync.dma_start(out=qs_sb[:], in_=qs.rearrange("(p t) o -> p (t o)", t=4))
-        share_sb = sb.tile([P, 2, 2], F32, name="share_sb")
-        nc.sync.dma_start(out=share_sb[:], in_=share.rearrange("(h p e) o -> p h (e o)", h=2, e=2))
-        g_raw = [load_half("g_raw0", grows, 0)]
+        share_sb = sb.tile([P, 2, 8], F32, name="share_sb")
+        nc.sync.dma_start(out=share_sb[:, :, 0:2], in_=share.rearrange("(h p e) o -> p h (e o)", h=2, e=2))
+        g_raw = load_whole("g_raw", grows)
+        old_sb = sb.tile([P, 2, 2, SLOTS], F32, name="old_sb")
+        nc.sync.dma_start(out=old_sb[:], in_=old.rearrange("(h p e) i -> p h e i", h=2, e=2))
         sg_col = sb.tile([P, 2], F32, name="sg_col")
         nc.sync.dma_start(out=sg_col[:], in_=sg.rearrange("o (p e) -> p (o e)", e=2))
-        g_raw.append(load_half("g_raw1", grows, 1))
-        old_sb = sb.tile([P, 2, 2 * SLOTS], F32, name="old_sb")
-        nc.sync.dma_start(out=old_sb[:], in_=old.rearrange("(h p e) i -> p h (e i)", h=2, e=2))
 
         warm = sb.tile([P, 1], F32, name="warm")
         warm_out = sb.tile([P, 1], F32, name="warm_out")
@@ -109,7 +112,7 @@ def tile_attend_bzcentred_soft_kernel(tc, query, keys_words, keys_scales, tab_wo
             return ap.rearrange("p e m j -> p (e m j)")
 
         neg_share = sb.tile([P, 2, 2], F32, name="neg_share")
-        nc.gpsimd.tensor_scalar(out=neg_share[:], in0=share_sb[:], scalar1=-1.0 / PAGE, scalar2=0.0, op0=ALU.mult, op1=ALU.add)
+        nc.gpsimd.tensor_scalar(out=neg_share[:], in0=share_sb[:, :, 0:2], scalar1=-1.0 / PAGE, scalar2=0.0, op0=ALU.mult, op1=ALU.add)
 
         def page_sums(name, values):
             sums = sb.tile([P, 2, PAGES], F32, name=name)
@@ -141,9 +144,10 @@ def tile_attend_bzcentred_soft_kernel(tc, query, keys_words, keys_scales, tab_wo
         key_scale = gather("key_scale", key_plane, U8)
         q_packed = sb.tile([P, 4, P, 4], BF16, name="q_packed", align_bytes=64)
         q_dst = q_packed[:].rearrange("p t m j -> p m j t")
-        q_src = [half[:].rearrange("p j (m t) -> p m j t", t=4) for half in q_raw]
-        nc.scalar.copy(out=q_dst[:, :64], in_=q_src[0])
-        nc.vector.tensor_copy(out=q_dst[:, 64:], in_=q_src[1])
+        q_src = q_raw[:].rearrange("p j (m t) -> p m j t", t=4)
+        split = 44
+        nc.scalar.copy(out=q_dst[:, :split], in_=q_src[:, :split])
+        nc.vector.tensor_copy(out=q_dst[:, split:], in_=q_src[:, split:])
         q_mx = [quantize("q0", merged(q_packed[:, 0:2]), 256)]
         key_mx = (gather("key_words", key_pool, U32), key_scale)
         q_mx.append(quantize("q1", merged(q_packed[:, 2:4]), 256))
@@ -196,9 +200,9 @@ def tile_attend_bzcentred_soft_kernel(tc, query, keys_words, keys_scales, tab_wo
             in_=weights[:].rearrange("p t (c i) -> p c t i", i=4),
         )
 
-        g_packed = [interleave_half("g_packed%d" % h, g_raw[h][:], ("neg_max1", None)[h]) for h in range(2)]
+        g_packed = [interleave_half("g_packed%d" % h, g_raw[:, :, 256 * h : 256 * (h + 1)], ("neg_max1", None)[h]) for h in range(2)]
         g_mx = [quantize("g0", merged(g_packed[0][:]), 256)]
-        wq_mx = quantize("wq", wq_packed[:].rearrange("p i t -> p (i t)"), SLOTS)
+        wq_mx = quantize("wq", wq_packed[:].rearrange("p i t -> p (i t)"), SLOTS, "neg_max1")
         pre.append(centre("pre1", 1, zh[1][:], zh_sums[1]))
         g_mx.append(quantize("g1", merged(g_packed[1][:]), 256))
 
@@ -213,32 +217,46 @@ def tile_attend_bzcentred_soft_kernel(tc, query, keys_words, keys_scales, tab_wo
             grads.append(c0)
 
         squares = []
-        hv_all = sb.tile([P, 2, 2, SLOTS], F32, name="hv", tag="g_raw1", align_bytes=64)
+        hv_all = sb.tile([P, 2, 2, SLOTS], F32, name="hv", tag="g_raw", align_bytes=64)
         for h in range(2):
             hv = hv_all[:, h]
             nc.scalar.activation(out=hv, in_=pre[h][:], func=ACT.Tanh)
             squares.append(sb.tile([P, 2, SLOTS], F32, name="sq%d" % h))
             nc.scalar.activation(out=squares[h][:], in_=hv, func=ACT.Square)
 
-        neg_u = []
-        for h in range(2):
-            neg_u.append(sb.tile([P, 2, SLOTS], F32, name="neg_u%d" % h))
+        def through_tanh(h):
+            neg_u = sb.tile([P, 2, SLOTS], F32, name="neg_u%d" % h)
             nc.vector.scalar_tensor_tensor(
-                out=neg_u[h][:].rearrange("p e i -> p (e i)"), in0=squares[h][:].rearrange("p e i -> p (e i)"), scalar=1.0,
+                out=neg_u[:].rearrange("p e i -> p (e i)"), in0=squares[h][:].rearrange("p e i -> p (e i)"), scalar=1.0,
                 in1=grads[h][:].rearrange("p e i -> p (e i)"), op0=ALU.subtract, op1=ALU.mult,
             )
-        u_sums = [page_sums("u_sums%d" % h, neg_u[h][:]) for h in range(2)]
-        neg_dzh = [centre("neg_dzh%d" % h, h, neg_u[h][:], u_sums[h]) for h in range(2)]
-        gained = []
-        for h in range(2):
-            gained.append(sb.tile([P, 2, SLOTS], F32, name="gained%d" % h))
+            return neg_u
+
+        def times_gain(name, neg_dzh, tiles):
+            gained = sb.tile([P, tiles, SLOTS], F32, name=name)
             nc.vector.tensor_tensor(
-                out=gained[h][:].rearrange("p e (n f) -> p e n f", f=2),
-                in0=neg_dzh[h][:].rearrange("p e (n f) -> p e n f", f=2),
-                in1=gain[:].rearrange("p f n -> p n f").unsqueeze(1).broadcast_to([P, 2, P, 2]),
+                out=gained[:].rearrange("p e (n f) -> p e n f", f=2),
+                in0=neg_dzh.rearrange("p e (n f) -> p e n f", f=2),
+                in1=gain[:].rearrange("p f n -> p n f").unsqueeze(1).broadcast_to([P, tiles, P, 2]),
                 op=ALU.mult,
             )
-        for h in range(2):
-            result = sb.tile([P, 2 * SLOTS], F32, name="result%d" % h)
-            nc.vector.tensor_tensor(out=result[:], in0=old_sb[:, h, :], in1=gained[h][:].rearrange("p e i -> p (e i)"), op=ALU.subtract)
-            nc.sync.dma_start(out=out[256 * h : 256 * (h + 1), :].rearrange("(p e) i -> p (e i)", e=2), in_=result[:])
+            return gained
+
+        out_rows = out.rearrange("(h p e) i -> p h e i", h=2, e=2)
+
+        def finish(name, h, tiles, gained, queue):
+            result = sb.tile([P, tiles.stop - tiles.start, SLOTS], F32, name=name)
+            nc.vector.tensor_tensor(out=result[:], in0=old_sb[:, h, tiles, :], in1=gained[:], op=ALU.subtract)
+            queue.dma_start(out=out_rows[:, h, tiles, :], in_=result[:])
+
+        neg_u0 = through_tanh(0)
+        u_sums0 = page_sums("u_sums0", neg_u0[:])
+        neg_u1 = through_tanh(1)
+        neg_dzh0 = centre("neg_dzh0", 0, neg_u0[:], u_sums0)
+        u_sums1 = page_sums("u_sums1", neg_u1[:])
+        gained0 = times_gain("gained0", neg_dzh0[:], 2)
+        neg_dzh1 = centre("neg_dzh1", 1, neg_u1[:], u_sums1)
+        finish("result0", 0, slice(0, 2), gained0, nc.sync)
+        gained1 = [times_gain("gained1_%d" % e, neg_dzh1[:, e : e + 1, :], 1) for e in range(2)]
+        for e, queue in enumerate((nc.sync, nc.sync)):
+            finish("result1_%d" % e, 1, slice(e, e + 1), gained1[e], queue)

from contextlib import ExitStack

import concourse.mybir as mybir
from concourse.masks import make_identity

F32 = mybir.dt.float32
BF16 = mybir.dt.bfloat16
I32 = mybir.dt.int32
U32 = mybir.dt.uint32
U16 = mybir.dt.uint16
U8 = mybir.dt.uint8
FP8X4 = mybir.dt.float8_e4m3fn_x4
ALU = mybir.AluOpType
ACT = mybir.ActivationFunctionType
AXIS_X = mybir.AxisListType.X

P = 128
T = 1024
SLOTS = 256
PAGE = 16
PAGES = SLOTS // PAGE
FLOPS = 3 * 2 * 512 * 512 * 256


def tile_attend_bzcentred_soft_kernel(tc, query, keys_words, keys_scales, tab_words, tab_scales, w1, share, qs, grows, sg, old, offs, out):
    nc = tc.nc
    with ExitStack() as ctx:
        sb = ctx.enter_context(tc.tile_pool(name="sb", bufs=1))
        ps = ctx.enter_context(tc.psum_pool(name="ps", bufs=1))

        def load_scales(name, scales, queue):
            plane = sb.tile([P, T], U8, name=name, align_bytes=64)
            rows = scales[0].bitcast(I32)
            for quad in range(4):
                queue.dma_start(
                    out=plane[32 * quad : 32 * quad + 32, :].bitcast(I32),
                    in_=rows[4 * quad : 4 * quad + 4, :].unsqueeze(0).broadcast_to([8, 4, T // 4]),
                )
            return plane

        def load_words(name, words):
            pool_words = sb.tile([P, T], U32, name=name, align_bytes=64)
            nc.sync.dma_start(out=pool_words[:].bitcast(I32), in_=words[0].rearrange("p n t -> p (n t)").bitcast(I32))
            return pool_words

        def load_half(name, matrix, h):
            half = sb.tile([P, 4, 256], F32, name=name, align_bytes=64)
            nc.sync.dma_start(out=half[:], in_=matrix[:, 256 * h : 256 * (h + 1)].rearrange("(p j) r -> p j r", j=4))
            return half

        def load_whole(name, matrix):
            whole = sb.tile([P, 4, 512], F32, name=name, align_bytes=64)
            nc.sync.dma_start(out=whole[:], in_=matrix.rearrange("(p j) r -> p j r", j=4))
            return whole

        def gather(name, window, dtype, tag=None):
            picked = sb.tile([P, SLOTS], dtype, name=name, tag=tag or name, align_bytes=64)
            nc.vector.tensor_copy(out=picked[:], in_=window[:].indirect(offsets[:]))
            return picked

        def quantize(name, values, width, tag=None):
            codes = sb.tile([P, width], U32, name=name + "_codes", tag=tag or name + "_codes", align_bytes=64)
            scales = sb.tile([P, width], U8, name=name + "_scales", align_bytes=64)
            nc.vector.quantize_mx(out=codes[:].bitcast(FP8X4), scales=scales[:], in_=values)
            return codes, scales

        def product(dst, stationary, col, moving):
            nc.tensor.matmul_mx(
                out=dst,
                lhsT=stationary[0][:, col * P : (col + 1) * P].bitcast(FP8X4),
                lhsT_scale=stationary[1][:, col * P : (col + 1) * P],
                rhs=moving[0][:].bitcast(FP8X4),
                rhs_scale=moving[1][:],
                start=True,
                stop=True,
            )

        def interleave_half(name, raw_half, tag=None):
            packed = sb.tile([P, 2, P, 4], BF16, name=name, tag=tag or name, align_bytes=64)
            dst = packed[:].rearrange("p e (m n) j -> p m j n e", n=2)
            src = raw_half.rearrange("p j (m n e) -> p m j n e", n=2, e=2)
            nc.scalar.copy(out=dst, in_=src)
            return packed

        offsets = sb.tile([P, SLOTS // 16], U16, name="offsets")
        nc.sync.dma_start(offsets[:], offs)
        key_plane = load_scales("key_plane", keys_scales, nc.sync)
        q_raw = load_whole("q_raw", query)
        key_pool = load_words("key_pool", keys_words)
        w_raw = [load_half("w_raw0", w1, 0)]
        tab_plane = load_scales("tab_plane", tab_scales, nc.sync)
        w_raw.append(load_half("w_raw1", w1, 1))
        tab_pool = load_words("tab_pool", tab_words)
        qs_sb = sb.tile([P, 4], F32, name="qs_sb")
        nc.sync.dma_start(out=qs_sb[:], in_=qs.rearrange("(p t) o -> p (t o)", t=4))
        share_sb = sb.tile([P, 2, 8], F32, name="share_sb")
        nc.sync.dma_start(out=share_sb[:, :, 0:2], in_=share.rearrange("(h p e) o -> p h (e o)", h=2, e=2))
        g_raw = load_whole("g_raw", grows)
        old_sb = sb.tile([P, 2, 2, SLOTS], F32, name="old_sb")
        nc.sync.dma_start(out=old_sb[:], in_=old.rearrange("(h p e) i -> p h e i", h=2, e=2))
        sg_col = sb.tile([P, 2], F32, name="sg_col")
        nc.sync.dma_start(out=sg_col[:], in_=sg.rearrange("o (p e) -> p (o e)", e=2))

        warm = sb.tile([P, 1], F32, name="warm")
        warm_out = sb.tile([P, 1], F32, name="warm_out")
        nc.vector.memset(warm[:], 0.0)
        nc.scalar.activation(out=warm_out[:], in_=warm[:], func=ACT.Exp)
        ident = sb.tile([P, P], F32, name="ident")
        make_identity(nc, ident[:])

        def merged(ap):
            return ap.rearrange("p e m j -> p (e m j)")

        neg_share = sb.tile([P, 2, 2], F32, name="neg_share")
        nc.gpsimd.tensor_scalar(out=neg_share[:], in0=share_sb[:, :, 0:2], scalar1=-1.0 / PAGE, scalar2=0.0, op0=ALU.mult, op1=ALU.add)

        def page_sums(name, values):
            sums = sb.tile([P, 2, PAGES], F32, name=name)
            nc.vector.tensor_reduce(
                out=sums[:].rearrange("p e g -> p (e g)"), in_=values.rearrange("p e (g j) -> p (e g) j", j=PAGE),
                axis=AXIS_X, op=ALU.add,
            )
            return sums

        def centre(name, h, values, sums):
            centred = sb.tile([P, 2, SLOTS], F32, name=name)
            for e in range(2):
                nc.vector.scalar_tensor_tensor(
                    out=centred[:, e, :].rearrange("p (g j) -> p g j", j=PAGE),
                    in0=sums[:, e, :].unsqueeze(2).broadcast_to([P, PAGES, PAGE]),
                    scalar=neg_share[:, h, e : e + 1],
                    in1=values[:, e, :].rearrange("p (g j) -> p g j", j=PAGE),
                    op0=ALU.mult, op1=ALU.add,
                )
            return centred


        def layer_sums(h, w_mx):
            sums_zh = ps.tile([P, 2, SLOTS], F32, name="zh%d" % h)
            for e in range(2):
                product(sums_zh[:, e, :], w_mx, e, tab_mx)
            return sums_zh

        key_scale = gather("key_scale", key_plane, U8)
        q_packed = sb.tile([P, 4, P, 4], BF16, name="q_packed", align_bytes=64)
        q_dst = q_packed[:].rearrange("p t m j -> p m j t")
        q_src = q_raw[:].rearrange("p j (m t) -> p m j t", t=4)
        split = 44
        nc.scalar.copy(out=q_dst[:, :split], in_=q_src[:, :split])
        nc.vector.tensor_copy(out=q_dst[:, split:], in_=q_src[:, split:])
        q_mx = [quantize("q0", merged(q_packed[:, 0:2]), 256)]
        key_mx = (gather("key_words", key_pool, U32), key_scale)
        q_mx.append(quantize("q1", merged(q_packed[:, 2:4]), 256))
        scores = [ps.tile([P, 2, SLOTS], F32, name="scores%d" % b) for b in range(2)]
        for t in range(4):
            product(scores[t // 2][:, t % 2, :], q_mx[t // 2], t % 2, key_mx)
        tab_scale = gather("tab_scale", tab_plane, U8)
        w_packed = [interleave_half("w_packed%d" % h, w_raw[h][:]) for h in range(2)]

        expd = sb.tile([P, 4, SLOTS], F32, name="expd", tag="w_raw1", align_bytes=64)
        row_sums = []
        for b in range(2):
            neg_max = sb.tile([P, 2], F32, name="neg_max%d" % b, tag=("tab_plane", "neg_max1")[b], align_bytes=64)
            nc.vector.tensor_reduce(out=neg_max[:], in_=scores[b][:], axis=AXIS_X, op=ALU.max, negate=True)
            row_sum = sb.tile([P, 2], F32, name="row_sum%d" % b)
            for e in range(2):
                nc.scalar.activation(
                    out=expd[:, 2 * b + e, :], in_=scores[b][:, e, :], func=ACT.Exp,
                    bias=neg_max[:, e : e + 1], accum_out=row_sum[:, e : e + 1],
                )
            row_sums.append(row_sum)

        weights = sb.tile([P, 4, SLOTS], BF16, name="weights")

        def invert(b, tag):
            inv_sum = sb.tile([P, 2], F32, name="inv_sum%d" % b, tag=tag, align_bytes=64)
            nc.vector.reciprocal(out=inv_sum[:], in_=row_sums[b][:])
            return inv_sum

        def normalise(b, inv_sum):
            for e in range(2):
                t = 2 * b + e
                nc.vector.tensor_scalar(
                    out=weights[:, t, :], in0=expd[:, t, :], scalar1=inv_sum[:, e : e + 1], scalar2=qs_sb[:, t : t + 1],
                    op0=ALU.mult, op1=ALU.mult,
                )

        w_mx0 = quantize("w0", merged(w_packed[0][:]), 256)
        tab_mx = (gather("tab_words", tab_pool, U32), tab_scale)
        zh = [layer_sums(0, w_mx0), layer_sums(1, quantize("w1", merged(w_packed[1][:]), 256))]
        normalise(0, invert(0, "tab_pool"))
        zh_sums = [page_sums("zh_sums0", zh[0][:])]
        inv_sum1 = invert(1, "inv_sum1")
        zh_sums.append(page_sums("zh_sums1", zh[1][:]))
        normalise(1, inv_sum1)
        pre = [centre("pre0", 0, zh[0][:], zh_sums[0])]
        wq_packed = sb.tile([P, SLOTS, 4], BF16, name="wq_packed", align_bytes=64)
        nc.vector.tensor_copy(
            out=wq_packed[:].rearrange("p (c i) t -> p c t i", i=4),
            in_=weights[:].rearrange("p t (c i) -> p c t i", i=4),
        )

        g_packed = [interleave_half("g_packed%d" % h, g_raw[:, :, 256 * h : 256 * (h + 1)], ("neg_max1", None)[h]) for h in range(2)]
        g_mx = [quantize("g0", merged(g_packed[0][:]), 256)]
        wq_mx = quantize("wq", wq_packed[:].rearrange("p i t -> p (i t)"), SLOTS, "neg_max1")
        pre.append(centre("pre1", 1, zh[1][:], zh_sums[1]))
        g_mx.append(quantize("g1", merged(g_packed[1][:]), 256))

        gain = ps.tile([P, 2, P], F32, name="gain", tag="scores1")
        for e in range(2):
            nc.tensor.transpose(gain[:, e, :], sg_col[:, e : e + 1].to_broadcast([P, P]), ident[:])
        grads = []
        for h in range(2):
            c0 = ps.tile([P, 2, SLOTS], F32, name="c0_%d" % h)
            for e in range(2):
                product(c0[:, e, :], g_mx[h], e, wq_mx)
            grads.append(c0)

        squares = []
        hv_all = sb.tile([P, 2, 2, SLOTS], F32, name="hv", tag="g_raw", align_bytes=64)
        for h in range(2):
            hv = hv_all[:, h]
            nc.scalar.activation(out=hv, in_=pre[h][:], func=ACT.Tanh)
            squares.append(sb.tile([P, 2, SLOTS], F32, name="sq%d" % h))
            nc.scalar.activation(out=squares[h][:], in_=hv, func=ACT.Square)

        def through_tanh(h):
            neg_u = sb.tile([P, 2, SLOTS], F32, name="neg_u%d" % h)
            nc.vector.scalar_tensor_tensor(
                out=neg_u[:].rearrange("p e i -> p (e i)"), in0=squares[h][:].rearrange("p e i -> p (e i)"), scalar=1.0,
                in1=grads[h][:].rearrange("p e i -> p (e i)"), op0=ALU.subtract, op1=ALU.mult,
            )
            return neg_u

        def times_gain(name, neg_dzh, tiles):
            gained = sb.tile([P, tiles, SLOTS], F32, name=name)
            nc.vector.tensor_tensor(
                out=gained[:].rearrange("p e (n f) -> p e n f", f=2),
                in0=neg_dzh.rearrange("p e (n f) -> p e n f", f=2),
                in1=gain[:].rearrange("p f n -> p n f").unsqueeze(1).broadcast_to([P, tiles, P, 2]),
                op=ALU.mult,
            )
            return gained

        out_rows = out.rearrange("(h p e) i -> p h e i", h=2, e=2)

        def finish(name, h, tiles, gained, queue):
            result = sb.tile([P, tiles.stop - tiles.start, SLOTS], F32, name=name)
            nc.vector.tensor_tensor(out=result[:], in0=old_sb[:, h, tiles, :], in1=gained[:], op=ALU.subtract)
            queue.dma_start(out=out_rows[:, h, tiles, :], in_=result[:])

        neg_u0 = through_tanh(0)
        u_sums0 = page_sums("u_sums0", neg_u0[:])
        neg_u1 = through_tanh(1)
        neg_dzh0 = centre("neg_dzh0", 0, neg_u0[:], u_sums0)
        u_sums1 = page_sums("u_sums1", neg_u1[:])
        gained0 = times_gain("gained0", neg_dzh0[:], 2)
        neg_dzh1 = centre("neg_dzh1", 1, neg_u1[:], u_sums1)
        finish("result0", 0, slice(0, 2), gained0, nc.sync)
        gained1 = [times_gain("gained1_%d" % e, neg_dzh1[:, e : e + 1, :], 1) for e in range(2)]
        for e, queue in enumerate((nc.sync, nc.sync)):
            finish("result1_%d" % e, 1, slice(e, e + 1), gained1[e], queue)
